import numpy as np
import ml_dtypes


def mxq(x, axis, fmt="e4m3"):
    dtype, down = {"e4m3": (ml_dtypes.float8_e4m3fn, 7), "e5m2": (ml_dtypes.float8_e5m2, 14)}[fmt]
    v = np.moveaxis(np.asarray(x, np.float32).astype(ml_dtypes.bfloat16).astype(np.float64), axis, -1)
    blocks = v.reshape(v.shape[:-1] + (-1, 32))
    amax = np.abs(blocks).max(-1, keepdims=True)
    byte = np.maximum(np.where(amax > 0, np.frexp(amax)[1] - 1 + 127, 0) - down, 1)
    scale = np.exp2(byte - 127.0)
    codes = (blocks / scale).astype(np.float32).astype(dtype).astype(np.float64)
    return np.moveaxis((codes * scale).reshape(v.shape), -1, axis)


WIDE = False


def mx_kscale(k):
    if not WIDE:
        return np.ones(k)
    levels = np.array([18, -18])
    if k % 512:
        return np.exp2(np.random.permutation(np.resize(levels, k // 32))).repeat(32)
    a = np.empty((k // 512, 16))
    for p in range(k // 512):
        a[p, :8] = np.random.permutation(np.resize(levels, 8))
        for g in range(8):
            far = levels[np.abs(levels - a[p, g]) >= 10]
            a[p, g + 8] = far[np.random.randint(len(far))]
    return np.exp2(a.ravel()).repeat(32)


def f64(x):
    return np.asarray(x).astype(np.float64)


def striped(idx):
    return np.tile(np.asarray(idx).reshape(-1, 16).T, (8, 1)).astype(np.uint16)


def unstriped(offs):
    return offs[:16].T.reshape(-1).astype(np.int64)


def sig(x):
    return 1.0 / (1.0 + np.exp(-x))


def setup_inputs():
    n = np.random.standard_normal
    uni = np.random.uniform
    src = np.random.permutation(np.repeat(np.arange(512), 2))
    outg = np.argsort(src, kind="stable")
    dst = np.random.randint(0, 512, 1024)
    f_d = mx_kscale(512)
    f_f = mx_kscale(512)
    return {
        "hT": (n((512, 512)) * f_f[:, None]).astype(np.float32),
        "W": (n((512, 512)) / np.sqrt(512) / f_f[:, None] * f_d[None, :]).astype(np.float32),
        "we": np.tile(uni(0.75, 1.3, 1024), (128, 1)).astype(np.float32),
        "y": np.tile(np.random.randint(0, 2, 1024), (128, 1)).astype(np.float32),
        "cd": (uni(0.15, 0.3, (512, 1)) / f_d[:, None]).astype(np.float32),
        "sx": np.tile(uni(0.75, 1.3, 512), (128, 1)).astype(np.float32),
        "srcoffs": striped(src),
        "outgoffs": striped(outg),
        "toffs": striped(dst),
    }


def reference(hT, W, we, y, cd, sx, srcoffs, outgoffs, toffs):
    src = unstriped(srcoffs)
    outg = unstriped(outgoffs)
    dst = unstriped(toffs)
    z0 = mxq(f64(W), 0, "e4m3").T @ mxq(f64(hT), 0, "e4m3")
    z = f64(cd) * f64(sx)[:1] * z0
    zs = z[:, src]
    zt = z[:, dst]
    q = zs * zt
    qt = q.T
    s = (qt).sum(-1, keepdims=True)
    sr = s.T
    g = f64(we)[:1] * (sig(sr) - f64(y)[:1])
    m = g * zt
    ms = m[:, outg]
    dz = ms.reshape(512, 512, 2).sum(-1)
    dv = f64(cd) * f64(sx)[:1] * dz
    out = mxq(f64(W), 1, "e4m3") @ mxq(dv, 0, "e5m2")
    return out

@@ -1,0 +1,330 @@
+from contextlib import ExitStack
+
+import concourse.mybir as mybir
+from concourse.masks import make_identity
+
+FLOPS = 2 * 2 * 512 * 512 * 512
+
+F32 = mybir.dt.float32
+BF16 = mybir.dt.bfloat16
+U32 = mybir.dt.uint32
+U16 = mybir.dt.uint16
+U8 = mybir.dt.uint8
+E4M3 = mybir.dt.float8_e4m3fn_x4
+E5M2 = mybir.dt.float8_e5m2_x4
+MULT = mybir.AluOpType.mult
+ADD = mybir.AluOpType.add
+COPY = mybir.ActivationFunctionType.Copy
+IDENTITY = mybir.ActivationFunctionType.Identity
+SIGMOID = mybir.ActivationFunctionType.Sigmoid
+
+P = 128
+PACK = 4
+NODES = 512
+EDGES = 1024
+Z_COLS = NODES + 16
+H_PIECES = [(0, 256), (256, 384), (384, 512)]
+EDGE_PIECES = [(0, 512), (512, 768), (768, 896), (896, 1024)]
+WE_ROW, Y_ROW, ROWS_END = 0, 8, 16
+
+
+def tile_attend_glink_kernel(tc, hT, W, we, y, cd, sx, srcoffs, outgoffs, toffs, out):
+    nc = tc.nc
+    with ExitStack() as ctx:
+        sb = ctx.enter_context(tc.tile_pool(name="sb", bufs=1))
+        ps = ctx.enter_context(tc.psum_pool(name="ps", bufs=1))
+
+        def bank(b, name):
+            return ps.tile([P, 512], F32, name=name, tag="bank%d" % b)
+
+        def offsets(tile, first, end):
+            return tile[:, first // 16 : end // 16]
+
+        cd_cols = sb.tile([P, PACK], F32, name="cd_cols")
+        nc.scalar.dma_start(out=cd_cols[:], in_=cd.rearrange("(p t) o -> p (t o)", t=PACK))
+        w_raw = sb.tile([P, PACK, 512], F32, name="w_raw")
+        nc.sync.dma_start(out=w_raw[:], in_=W.rearrange("(p j) d -> p j d", j=PACK))
+        h_raw = []
+        for n, (a, b) in enumerate(H_PIECES):
+            piece = sb.tile([P, PACK, b - a], F32, name="h_raw%d" % n)
+            nc.sync.dma_start(out=piece[:], in_=hT.rearrange("(p j) x -> p j x", j=PACK)[:, :, a:b])
+            h_raw.append(piece)
+
+        sx_all = sb.tile([P, NODES], F32, name="sx_all")
+        nc.sync.dma_start(out=sx_all[:], in_=sx)
+        dst_list = sb.tile([P, EDGES // 16], U16, name="dst_list")
+        nc.sync.dma_start(out=dst_list[:], in_=toffs)
+        src_list = sb.tile([P, EDGES // 16], U16, name="src_list")
+        nc.sync.dma_start(out=src_list[:], in_=srcoffs)
+        outg_list = sb.tile([P, EDGES // 16], U16, name="outg_list")
+        nc.sync.dma_start(out=outg_list[:], in_=outgoffs)
+
+        ident = sb.tile([P, P], F32, name="ident")
+        make_identity(nc, ident[:])
+        rows = sb.tile([P, P], F32, name="rows")
+        nc.gpsimd.memset(rows[:], 0.0)
+        nc.sync.dma_start(out=rows[WE_ROW:Y_ROW, :], in_=we[0:1, :].rearrange("o (k n) -> (o k) n", n=P))
+        nc.sync.dma_start(out=rows[Y_ROW:ROWS_END, :], in_=y[0:1, :].rearrange("o (k n) -> (o k) n", n=P))
+        z = [sb.tile([P, Z_COLS], F32, name="z%d" % t) for t in range(PACK)]
+        for t in range(PACK):
+            nc.gpsimd.memset(z[t][:, NODES:Z_COLS], 0.0)
+
+        w_bf = sb.tile([P, PACK, P, PACK], BF16, name="w_bf", align_bytes=64)
+        w_src = w_raw[:].rearrange("p j (m t) -> p m j t", t=PACK)
+        w_dst = w_bf[:].rearrange("p t m j -> p m j t")
+        w_codes = sb.tile([P, 512], U32, name="w_codes", align_bytes=64)
+        w_scales = sb.tile([P, 512], U8, name="w_scales", align_bytes=64)
+        nc.vector.tensor_copy(out=w_dst[:, :, :, 0:2], in_=w_src[:, :, :, 0:2])
+        nc.scalar.copy(out=w_dst[:, :, :, 2:4], in_=w_src[:, :, :, 2:4])
+
+        def quantize_w(half):
+            c = slice(256 * half, 256 * (half + 1))
+            nc.vector.quantize_mx(
+                out=w_codes[:, c].bitcast(E4M3),
+                scales=w_scales[:, c],
+                in_=w_bf[:, 2 * half : 2 * half + 2].rearrange("p t m j -> p (t m j)"),
+            )
+
+        h_codes = sb.tile([P, NODES], U32, name="h_codes", align_bytes=64)
+        h_scales = sb.tile([P, NODES], U8, name="h_scales", align_bytes=64)
+        h_bf = [sb.tile([P, b - a, PACK], BF16, name="h_bf%d" % n, align_bytes=64) for n, (a, b) in enumerate(H_PIECES)]
+
+        def cast_h(n, copy):
+            copy(
+                out=h_bf[n][:].rearrange("p (c i) j -> p c j i", i=4),
+                in_=h_raw[n][:].rearrange("p j (c i) -> p c j i", i=4),
+            )
+
+        def quantize_h(n):
+            a, b = H_PIECES[n]
+            nc.vector.quantize_mx(
+                out=h_codes[:, a:b].bitcast(E4M3),
+                scales=h_scales[:, a:b],
+                in_=h_bf[n][:].rearrange("p x j -> p (x j)"),
+            )
+
+        def mx(out_ap, codes_l, scales_l, cl, codes_r, scales_r, cr, fmt_r=E4M3):
+            nc.tensor.matmul_mx(
+                out=out_ap,
+                lhsT=codes_l[:, cl].bitcast(E4M3),
+                lhsT_scale=scales_l[:, cl],
+                rhs=codes_r[:, cr].bitcast(fmt_r),
+                rhs_scale=scales_r[:, cr],
+                start=True,
+                stop=True,
+            )
+
+        def plane0(n, b):
+            lo, hi = H_PIECES[n]
+            acc = bank(b, "z0_ps%d" % n)
+            mx(acc[:, 0 : hi - lo], w_codes, w_scales, slice(0, P), h_codes, h_scales, slice(lo, hi))
+            nc.vector.scalar_tensor_tensor(
+                out=z[0][:, lo:hi], in0=acc[:, 0 : hi - lo], scalar=cd_cols[:, 0:1], in1=sx_all[:, lo:hi], op0=MULT, op1=MULT
+            )
+
+        quantize_w(0)
+        cast_h(0, nc.vector.tensor_copy)
+        quantize_w(1)
+        quantize_h(0)
+        cast_h(1, nc.scalar.copy)
+        cast_h(2, nc.vector.tensor_copy)
+        quantize_h(1)
+        quantize_h(2)
+        plane0(0, 2)
+        plane0(1, 0)
+        plane0(2, 1)
+
+        sx_ps = bank(5, "sx_ps")
+        for k in range(4):
+            nc.tensor.transpose(sx_ps[:, k * P : (k + 1) * P], sx_all[:, k * P : (k + 1) * P], ident[:])
+        sx_cols = sb.tile([P, 4], F32, name="sx_cols")
+        nc.scalar.copy(out=sx_cols[:], in_=sx_ps[:, 0:NODES:P])
+        back = [None] + [bank(4 + t, "z_back%d" % t) for t in range(1, PACK)]
+        z_nodes = []
+        for k in range(4):
+            acc = bank(3 + k % 2, "zt_ps%d" % k)
+            nodes = slice(k * P, (k + 1) * P)
+            mx(acc[:, 0:128], h_codes, h_scales, nodes, w_codes, w_scales, slice(128, 256))
+            mx(acc[:, 128:384], h_codes, h_scales, nodes, w_codes, w_scales, slice(256, 512))
+            scaled = sb.tile([P, 384], F32, name="z_nodes%d" % k)
+            nc.scalar.activation(out=scaled[:], in_=acc[:, 0:384], func=COPY, scale=sx_cols[:, k : k + 1])
+            z_nodes.append(scaled)
+        for t in range(1, PACK):
+            for k in range(4):
+                nc.tensor.transpose(back[t][:, k * P : (k + 1) * P], z_nodes[k][:, (t - 1) * P : t * P], ident[:])
+            nc.scalar.activation(out=z[t][:, 0:NODES], in_=back[t][:], func=COPY, scale=cd_cols[:, t : t + 1])
+
+        w_words = w_bf[:].rearrange("p t m j -> p (t m j)").bitcast(F32).rearrange("p (t m u) -> p t m u", t=4, u=2)
+        wt_bf = sb.tile([P, PACK, P, PACK], BF16, name="wt_bf", align_bytes=64)
+        for u in range(2):
+            turned = bank(6 + u, "wt_ps%d" % u)
+            for t in range(PACK):
+                nc.tensor.transpose(turned[:, t * P : (t + 1) * P], w_words[:, t, :, u], ident[:])
+            nc.scalar.copy(
+                out=wt_bf[:, 2 * u : 2 * u + 2],
+                in_=turned[:].bitcast(BF16).rearrange("m (t p e) -> m e p t", t=4, e=2),
+            )
+        wt_codes = sb.tile([P, 512], U32, name="wt_codes", align_bytes=64)
+        wt_scales = sb.tile([P, 512], U8, name="wt_scales", align_bytes=64)
+
+        rows_t = bank(5, "rows_t")
+        nc.tensor.transpose(rows_t[:, 0:P], rows[:], ident[:])
+        we_cols = sb.tile([P, 8], F32, name="we_cols")
+        nc.scalar.copy(out=we_cols[:], in_=rows_t[:, WE_ROW:Y_ROW])
+        neg_wy = sb.tile([P, 8], F32, name="neg_wy")
+        nc.vector.scalar_tensor_tensor(
+            out=neg_wy[:], in0=rows_t[:, Y_ROW:ROWS_END], scalar=-1.0, in1=we_cols[:], op0=MULT, op1=MULT
+        )
+
+        last = slice(NODES - P, NODES)
+        cd_sx = sb.tile([P, P // 4, PACK, 4], F32, name="cd_sx")
+        for t in range(PACK):
+            nc.scalar.activation(
+                out=cd_sx[:, :, t, :],
+                in_=sx_all[:, last].rearrange("p (c i) -> p c i", i=4),
+                func=COPY,
+                scale=cd_cols[:, t : t + 1],
+            )
+
+        z_dst = sb.tile([P, PACK, EDGES], F32, name="z_dst")
+        q = sb.tile([P, PACK, EDGES], F32, name="q")
+        m = sb.tile([P, PACK, EDGES], F32, name="m")
+
+        def gather_dst(t, a, b):
+            nc.vector.tensor_copy(z_dst[:, t, a:b], z[t][:].indirect(offsets(dst_list, a, b)))
+
+        def gather_src(t, a, b):
+            nc.vector.tensor_tensor(q[:, t, a:b], z[t][:].indirect(offsets(src_list, a, b)), z_dst[:, t, a:b], MULT)
+
+        for a in (0, 512):
+            gather_dst(0, a, a + 512)
+        for a in (0, 512):
+            gather_src(0, a, a + 512)
+
+        s = sb.tile([P, 8], F32, name="s")
+        sig = sb.tile([P, 8], F32, name="sig")
+        g = sb.tile([P, 8], F32, name="g")
+        unread = sb.tile([P, P], F32, name="unread")
+
+        def score(n, q_bank):
+            a, b = EDGE_PIECES[n]
+            gather_dst(1, a, b)
+            gather_dst(2, a, b)
+            gather_src(1, a, b)
+            gather_dst(3, a, b)
+            gather_src(2, a, b)
+            gather_src(3, a, b)
+            q_ps = bank(q_bank, "q_ps%d" % n)
+            chunks = range(a // P, b // P)
+            for k in chunks:
+                part = q_ps[:, k * P - a : (k + 1) * P - a]
+                order = (3, 0, 1, 2) if k == 0 else (0, 1, 2, 3)
+                for t in order:
+                    nc.tensor.matmul(
+                        part, q[:, t, k * P : (k + 1) * P], ident[:], start=(t == order[0]), stop=(t == order[3]), is_transpose=True
+                    )
+            for k in chunks:
+                part = q_ps[:, k * P - a : (k + 1) * P - a]
+                nc.scalar.activation(out=unread[:], in_=part, func=IDENTITY, accum_out=s[:, k : k + 1])
+            nc.scalar.activation(out=sig[:, a // P : b // P], in_=s[:, a // P : b // P], func=SIGMOID)
+            for k in chunks:
+                nc.scalar.activation(
+                    out=g[:, k : k + 1], in_=sig[:, k : k + 1], func=IDENTITY, scale=we_cols[:, k : k + 1], bias=neg_wy[:, k : k + 1]
+                )
+
+        def spread_g(n, g_bank):
+            a, b = EDGE_PIECES[n]
+            spread = bank(g_bank, "g_ps%d" % n)
+            for k in range(a // P, b // P):
+                nc.tensor.transpose(spread[:, k * P - a : (k + 1) * P - a], g[:, k : k + 1].to_broadcast([P, P]), ident[:])
+            return spread
+
+        def m_by_turning(k):
+            edges = slice(k * P, (k + 1) * P)
+            turned = bank(3 + k % 2, "zd_ps%d" % k)
+            for t in range(PACK):
+                nc.tensor.transpose(turned[:, t * P : (t + 1) * P], z_dst[:, t, edges], ident[:])
+            m_edges = sb.tile([P, PACK * P], F32, name="m_edges%d" % k)
+            nc.scalar.activation(out=m_edges[:], in_=turned[:], func=COPY, scale=g[:, k : k + 1])
+            m_ps = bank(5 + k % 2, "m_ps%d" % k)
+            for t in range(PACK):
+                nc.tensor.transpose(m_ps[:, t * P : (t + 1) * P], m_edges[:, t * P : (t + 1) * P], ident[:])
+            nc.scalar.copy(out=m[:, :, edges], in_=m_ps[:].rearrange("p (t c) -> p t c", t=PACK))
+
+        def m_direct(n, spread):
+            a, b = EDGE_PIECES[n]
+            nc.vector.tensor_tensor(
+                m[:, :, a:b], z_dst[:, :, a:b], spread[:, 0 : b - a].unsqueeze(1).to_broadcast([P, PACK, b - a]), MULT
+            )
+
+        spreads = []
+        for n in range(len(EDGE_PIECES)):
+            score(n, 0)
+            spreads.append(spread_g(n, (5, 6, 7, 2)[n]))
+        nc.vector.quantize_mx(
+            out=wt_codes[:].bitcast(E4M3), scales=wt_scales[:], in_=wt_bf[:].rearrange("m j p t -> m (j p t)")
+        )
+        for n in range(len(EDGE_PIECES)):
+            m_direct(n, spreads[n])
+
+        dv_codes = sb.tile([P, NODES], U32, name="dv_codes", align_bytes=64)
+        dv_scales = sb.tile([P, NODES], U8, name="dv_scales", align_bytes=64)
+        dv_bf = [sb.tile([P, P * PACK], BF16, name="dv_bf%d" % k, align_bytes=64) for k in range(4)]
+
+        def quantize_dv(k):
+            nodes = slice(k * P, (k + 1) * P)
+            nc.vector.quantize_mx(out=dv_codes[:, nodes].bitcast(E5M2), scales=dv_scales[:, nodes], in_=dv_bf[k][:])
+
+        for k in range(3):
+            dz_ps = bank(3 + k % 2, "dz_ps%d" % k)
+            for t in range(PACK):
+                picked = sb.tile([P, 2 * P], F32, name="picked%d_%d" % (k, t))
+                nc.vector.tensor_copy(picked[:], m[:, t, :].indirect(offsets(outg_list, 2 * P * k, 2 * P * (k + 1))))
+                scaled = sb.tile([P, 2, P], F32, name="picked_cd%d_%d" % (k, t))
+                nc.scalar.activation(
+                    out=scaled[:], in_=picked[:].rearrange("p (x j) -> p j x", j=2), func=COPY, scale=cd_cols[:, t : t + 1]
+                )
+                for j in range(2):
+                    nc.tensor.matmul(
+                        dz_ps[:, t * P : (t + 1) * P], scaled[:, j, :], ident[:], start=(j == 0), stop=(j == 1), is_transpose=True
+                    )
+            dv_nodes = sb.tile([P, 2, P, 2], BF16, name="dv_nodes%d" % k)
+            nc.scalar.activation(
+                out=dv_nodes[:], in_=dz_ps[:].rearrange("x (u e p) -> x u p e", u=2, e=2), func=COPY, scale=sx_cols[:, k : k + 1]
+            )
+            words = dv_nodes[:].rearrange("x u p e -> x (u p e)").bitcast(F32)
+            dv_ps = bank((0, 5)[k % 2], "dv_ps%d" % k)
+            for u in range(2):
+                nc.tensor.transpose(dv_ps[:, u * P : (u + 1) * P], words[:, u * P : (u + 1) * P], ident[:])
+            nc.scalar.copy(
+                out=dv_bf[k][:].bitcast(F32).rearrange("p (x u) -> p x u", u=2),
+                in_=dv_ps[:, 0 : 2 * P].rearrange("p (u x) -> p x u", u=2),
+            )
+
+        picked_last = sb.tile([P, PACK, 2 * P], F32, name="picked_last")
+        for t in range(PACK):
+            nc.vector.tensor_copy(picked_last[:, t, :], m[:, t, :].indirect(offsets(outg_list, 2 * P * 3, EDGES)))
+        pairs = picked_last[:].rearrange("p t (x j) -> p (t x) j", j=2)
+        dz_last = sb.tile([P, PACK, P], F32, name="dz_last")
+        quantize_dv(0)
+        nc.vector.tensor_tensor(dz_last[:].rearrange("p t x -> p (t x)"), pairs[:, :, 0], pairs[:, :, 1], ADD)
+        quantize_dv(1)
+        nc.vector.tensor_tensor(
+            dv_bf[3][:].rearrange("p (c i t) -> p c t i", i=4, t=4),
+            dz_last[:].rearrange("p t (c i) -> p c t i", i=4),
+            cd_sx[:],
+            MULT,
+        )
+        quantize_dv(2)
+        quantize_dv(3)
+
+        out_rows = out.rearrange("(p j) x -> p j x", j=PACK)
+        for j in range(PACK):
+            acc = bank((5, 6, 7, 2)[j], "out_ps%d" % j)
+            mx(acc[:], wt_codes, wt_scales, slice(j * P, (j + 1) * P), dv_codes, dv_scales, slice(0, NODES), E5M2)
+            result = sb.tile([P, NODES], F32, name="result%d" % j)
+            if j % 2 == 0:
+                nc.scalar.copy(out=result[:], in_=acc[:])
+            else:
+                nc.vector.tensor_copy(out=result[:], in_=acc[:])
+            nc.sync.dma_start(out=out_rows[:, j, :], in_=result[:])

@@ -24,7 +24,7 @@ NODES = 512
 EDGES = 1024
 Z_COLS = NODES + 16
 H_PIECES = [(0, 256), (256, 384), (384, 512)]
-EDGE_PIECES = [(0, 512), (512, 768), (768, 896), (896, 1024)]
+EDGE_PIECES = [(0, 256), (256, 512), (512, 768), (768, 896), (896, 1024)]
 WE_ROW, Y_ROW, ROWS_END = 0, 8, 16
 
 
@@ -65,11 +65,11 @@ def tile_attend_glink_kernel(tc, hT, W, we, y, cd, sx, srcoffs, outgoffs, toffs,
         nc.gpsimd.memset(rows[:], 0.0)
         nc.sync.dma_start(out=rows[WE_ROW:Y_ROW, :], in_=we[0:1, :].rearrange("o (k n) -> (o k) n", n=P))
         nc.sync.dma_start(out=rows[Y_ROW:ROWS_END, :], in_=y[0:1, :].rearrange("o (k n) -> (o k) n", n=P))
-        z = [sb.tile([P, Z_COLS], F32, name="z%d" % t) for t in range(PACK)]
+        z = [sb.tile([P, Z_COLS], F32, name="z%d" % t, tag="z%d" % t) for t in range(PACK)]
         for t in range(PACK):
             nc.gpsimd.memset(z[t][:, NODES:Z_COLS], 0.0)
 
-        w_bf = sb.tile([P, PACK, P, PACK], BF16, name="w_bf", align_bytes=64)
+        w_bf = sb.tile([P, PACK, P, PACK], BF16, name="w_bf", tag="w_bf", align_bytes=64)
         w_src = w_raw[:].rearrange("p j (m t) -> p m j t", t=PACK)
         w_dst = w_bf[:].rearrange("p t m j -> p m j t")
         w_codes = sb.tile([P, 512], U32, name="w_codes", align_bytes=64)
@@ -176,19 +176,18 @@ def tile_attend_glink_kernel(tc, hT, W, we, y, cd, sx, srcoffs, outgoffs, toffs,
             out=neg_wy[:], in0=rows_t[:, Y_ROW:ROWS_END], scalar=-1.0, in1=we_cols[:], op0=MULT, op1=MULT
         )
 
-        last = slice(NODES - P, NODES)
-        cd_sx = sb.tile([P, P // 4, PACK, 4], F32, name="cd_sx")
+        factors = sb.tile([P, 2, PACK, 2 * P], F32, name="factors", tag="w_bf", align_bytes=64)
+        nc.scalar.copy(out=factors[:, 0], in_=cd_cols[:].unsqueeze(2).to_broadcast([P, PACK, 2 * P]))
         for t in range(PACK):
             nc.scalar.activation(
-                out=cd_sx[:, :, t, :],
-                in_=sx_all[:, last].rearrange("p (c i) -> p c i", i=4),
+                out=factors[:, 1, t, :].rearrange("p (x j) -> p x j", j=2),
+                in_=sx_all[:, NODES - P : NODES].unsqueeze(2).to_broadcast([P, P, 2]),
                 func=COPY,
                 scale=cd_cols[:, t : t + 1],
             )
 
         z_dst = sb.tile([P, PACK, EDGES], F32, name="z_dst")
-        q = sb.tile([P, PACK, EDGES], F32, name="q")
-        m = sb.tile([P, PACK, EDGES], F32, name="m")
+        q = sb.tile([P, PACK, EDGES], F32, name="q", tag="q")
 
         def gather_dst(t, a, b):
             nc.vector.tensor_copy(z_dst[:, t, a:b], z[t][:].indirect(offsets(dst_list, a, b)))
@@ -204,7 +203,7 @@ def tile_attend_glink_kernel(tc, hT, W, we, y, cd, sx, srcoffs, outgoffs, toffs,
         s = sb.tile([P, 8], F32, name="s")
         sig = sb.tile([P, 8], F32, name="sig")
         g = sb.tile([P, 8], F32, name="g")
-        unread = sb.tile([P, P], F32, name="unread")
+        unread = sb.tile([P, 8, P], F32, name="unread")
 
         def score(n, q_bank):
             a, b = EDGE_PIECES[n]
@@ -225,7 +224,7 @@ def tile_attend_glink_kernel(tc, hT, W, we, y, cd, sx, srcoffs, outgoffs, toffs,
                     )
             for k in chunks:
                 part = q_ps[:, k * P - a : (k + 1) * P - a]
-                nc.scalar.activation(out=unread[:], in_=part, func=IDENTITY, accum_out=s[:, k : k + 1])
+                nc.scalar.activation(out=unread[:, k, :], in_=part, func=IDENTITY, accum_out=s[:, k : k + 1])
             nc.scalar.activation(out=sig[:, a // P : b // P], in_=s[:, a // P : b // P], func=SIGMOID)
             for k in chunks:
                 nc.scalar.activation(
@@ -239,33 +238,28 @@ def tile_attend_glink_kernel(tc, hT, W, we, y, cd, sx, srcoffs, outgoffs, toffs,
                 nc.tensor.transpose(spread[:, k * P - a : (k + 1) * P - a], g[:, k : k + 1].to_broadcast([P, P]), ident[:])
             return spread
 
-        def m_by_turning(k):
-            edges = slice(k * P, (k + 1) * P)
-            turned = bank(3 + k % 2, "zd_ps%d" % k)
-            for t in range(PACK):
-                nc.tensor.transpose(turned[:, t * P : (t + 1) * P], z_dst[:, t, edges], ident[:])
-            m_edges = sb.tile([P, PACK * P], F32, name="m_edges%d" % k)
-            nc.scalar.activation(out=m_edges[:], in_=turned[:], func=COPY, scale=g[:, k : k + 1])
-            m_ps = bank(5 + k % 2, "m_ps%d" % k)
-            for t in range(PACK):
-                nc.tensor.transpose(m_ps[:, t * P : (t + 1) * P], m_edges[:, t * P : (t + 1) * P], ident[:])
-            nc.scalar.copy(out=m[:, :, edges], in_=m_ps[:].rearrange("p (t c) -> p t c", t=PACK))
-
-        def m_direct(n, spread):
-            a, b = EDGE_PIECES[n]
-            nc.vector.tensor_tensor(
-                m[:, :, a:b], z_dst[:, :, a:b], spread[:, 0 : b - a].unsqueeze(1).to_broadcast([P, PACK, b - a]), MULT
-            )
-
+        g_rows = sb.tile([P, 512], F32, name="g_rows")
         spreads = []
-        for n in range(len(EDGE_PIECES)):
+        for n, (a, b) in enumerate(EDGE_PIECES):
             score(n, 0)
-            spreads.append(spread_g(n, (5, 6, 7, 2)[n]))
-        nc.vector.quantize_mx(
-            out=wt_codes[:].bitcast(E4M3), scales=wt_scales[:], in_=wt_bf[:].rearrange("m j p t -> m (j p t)")
-        )
-        for n in range(len(EDGE_PIECES)):
-            m_direct(n, spreads[n])
+            spreads.append(spread_g(n, (5, 6, 7, 2, 1)[n]))
+            if b <= 512:
+                nc.scalar.copy(out=g_rows[:, a:b], in_=spreads[n][:, 0 : b - a])
+            if n == 1:
+                nc.vector.quantize_mx(
+                    out=wt_codes[:].bitcast(E4M3), scales=wt_scales[:], in_=wt_bf[:].rearrange("m j p t -> m (j p t)")
+                )
+
+        m = [sb.tile([P, EDGES], F32, name="m%d" % t, tag=tag) for t, tag in enumerate(("m0", "m1", "z3", "q"))]
+        gpsimd_end = (0, 0, 512, 512)
+        for t in (2, 3):
+            e = gpsimd_end[t]
+            nc.gpsimd.tensor_tensor(m[t][:, 0:e], z_dst[:, t, 0:e], g_rows[:, 0:e], MULT)
+        for n, (a, b) in enumerate(EDGE_PIECES):
+            for t in range(PACK):
+                first = max(a, gpsimd_end[t])
+                if first < b:
+                    nc.vector.tensor_tensor(m[t][:, first:b], z_dst[:, t, first:b], spreads[n][:, first - a : b - a], MULT)
 
         dv_codes = sb.tile([P, NODES], U32, name="dv_codes", align_bytes=64)
         dv_scales = sb.tile([P, NODES], U8, name="dv_scales", align_bytes=64)
@@ -275,18 +269,17 @@ def tile_attend_glink_kernel(tc, hT, W, we, y, cd, sx, srcoffs, outgoffs, toffs,
             nodes = slice(k * P, (k + 1) * P)
             nc.vector.quantize_mx(out=dv_codes[:, nodes].bitcast(E5M2), scales=dv_scales[:, nodes], in_=dv_bf[k][:])
 
+        def gather_outg(picked, t, k, factor):
+            nc.vector.tensor_tensor(picked, m[t][:].indirect(offsets(outg_list, 2 * P * k, 2 * P * (k + 1))), factor, MULT)
+
         for k in range(3):
             dz_ps = bank(3 + k % 2, "dz_ps%d" % k)
             for t in range(PACK):
                 picked = sb.tile([P, 2 * P], F32, name="picked%d_%d" % (k, t))
-                nc.vector.tensor_copy(picked[:], m[:, t, :].indirect(offsets(outg_list, 2 * P * k, 2 * P * (k + 1))))
-                scaled = sb.tile([P, 2, P], F32, name="picked_cd%d_%d" % (k, t))
-                nc.scalar.activation(
-                    out=scaled[:], in_=picked[:].rearrange("p (x j) -> p j x", j=2), func=COPY, scale=cd_cols[:, t : t + 1]
-                )
+                gather_outg(picked[:], t, k, factors[:, 0, t, :])
                 for j in range(2):
                     nc.tensor.matmul(
-                        dz_ps[:, t * P : (t + 1) * P], scaled[:, j, :], ident[:], start=(j == 0), stop=(j == 1), is_transpose=True
+                        dz_ps[:, t * P : (t + 1) * P], picked[:, j : 2 * P : 2], ident[:], start=(j == 0), stop=(j == 1), is_transpose=True
                     )
             dv_nodes = sb.tile([P, 2, P, 2], BF16, name="dv_nodes%d" % k)
             nc.scalar.activation(
@@ -303,18 +296,13 @@ def tile_attend_glink_kernel(tc, hT, W, we, y, cd, sx, srcoffs, outgoffs, toffs,
 
         picked_last = sb.tile([P, PACK, 2 * P], F32, name="picked_last")
         for t in range(PACK):
-            nc.vector.tensor_copy(picked_last[:, t, :], m[:, t, :].indirect(offsets(outg_list, 2 * P * 3, EDGES)))
-        pairs = picked_last[:].rearrange("p t (x j) -> p (t x) j", j=2)
-        dz_last = sb.tile([P, PACK, P], F32, name="dz_last")
+            gather_outg(picked_last[:, t, :], t, 3, factors[:, 1, t, :])
+        pairs = picked_last[:].rearrange("p t (c i j) -> p c t i j", i=4, j=2)
         quantize_dv(0)
-        nc.vector.tensor_tensor(dz_last[:].rearrange("p t x -> p (t x)"), pairs[:, :, 0], pairs[:, :, 1], ADD)
-        quantize_dv(1)
         nc.vector.tensor_tensor(
-            dv_bf[3][:].rearrange("p (c i t) -> p c t i", i=4, t=4),
-            dz_last[:].rearrange("p t (c i) -> p c t i", i=4),
-            cd_sx[:],
-            MULT,
+            dv_bf[3][:].rearrange("p (c i t) -> p c t i", i=4, t=4), pairs[:, :, :, :, 0], pairs[:, :, :, :, 1], ADD
         )
+        quantize_dv(1)
         quantize_dv(2)
         quantize_dv(3)
 

from contextlib import ExitStack

import concourse.mybir as mybir
from concourse.masks import make_identity

FLOPS = 2 * 2 * 512 * 512 * 512

F32 = mybir.dt.float32
BF16 = mybir.dt.bfloat16
U32 = mybir.dt.uint32
U16 = mybir.dt.uint16
U8 = mybir.dt.uint8
E4M3 = mybir.dt.float8_e4m3fn_x4
E5M2 = mybir.dt.float8_e5m2_x4
MULT = mybir.AluOpType.mult
ADD = mybir.AluOpType.add
COPY = mybir.ActivationFunctionType.Copy
IDENTITY = mybir.ActivationFunctionType.Identity
SIGMOID = mybir.ActivationFunctionType.Sigmoid

P = 128
PACK = 4
NODES = 512
EDGES = 1024
Z_COLS = NODES + 16
H_PIECES = [(0, 256), (256, 384), (384, 512)]
EDGE_PIECES = [(0, 256), (256, 512), (512, 768), (768, 896), (896, 1024)]
WE_ROW, Y_ROW, ROWS_END = 0, 8, 16


def tile_attend_glink_kernel(tc, hT, W, we, y, cd, sx, srcoffs, outgoffs, toffs, out):
    nc = tc.nc
    with ExitStack() as ctx:
        sb = ctx.enter_context(tc.tile_pool(name="sb", bufs=1))
        ps = ctx.enter_context(tc.psum_pool(name="ps", bufs=1))

        def bank(b, name):
            return ps.tile([P, 512], F32, name=name, tag="bank%d" % b)

        def offsets(tile, first, end):
            return tile[:, first // 16 : end // 16]

        cd_cols = sb.tile([P, PACK], F32, name="cd_cols")
        nc.scalar.dma_start(out=cd_cols[:], in_=cd.rearrange("(p t) o -> p (t o)", t=PACK))
        w_raw = sb.tile([P, PACK, 512], F32, name="w_raw")
        nc.sync.dma_start(out=w_raw[:], in_=W.rearrange("(p j) d -> p j d", j=PACK))
        h_raw = []
        for n, (a, b) in enumerate(H_PIECES):
            piece = sb.tile([P, PACK, b - a], F32, name="h_raw%d" % n)
            nc.sync.dma_start(out=piece[:], in_=hT.rearrange("(p j) x -> p j x", j=PACK)[:, :, a:b])
            h_raw.append(piece)

        sx_all = sb.tile([P, NODES], F32, name="sx_all")
        nc.sync.dma_start(out=sx_all[:], in_=sx)
        dst_list = sb.tile([P, EDGES // 16], U16, name="dst_list")
        nc.sync.dma_start(out=dst_list[:], in_=toffs)
        src_list = sb.tile([P, EDGES // 16], U16, name="src_list")
        nc.sync.dma_start(out=src_list[:], in_=srcoffs)
        outg_list = sb.tile([P, EDGES // 16], U16, name="outg_list")
        nc.sync.dma_start(out=outg_list[:], in_=outgoffs)

        ident = sb.tile([P, P], F32, name="ident")
        make_identity(nc, ident[:])
        rows = sb.tile([P, P], F32, name="rows")
        nc.gpsimd.memset(rows[:], 0.0)
        nc.sync.dma_start(out=rows[WE_ROW:Y_ROW, :], in_=we[0:1, :].rearrange("o (k n) -> (o k) n", n=P))
        nc.sync.dma_start(out=rows[Y_ROW:ROWS_END, :], in_=y[0:1, :].rearrange("o (k n) -> (o k) n", n=P))
        z = [sb.tile([P, Z_COLS], F32, name="z%d" % t, tag="z%d" % t) for t in range(PACK)]
        for t in range(PACK):
            nc.gpsimd.memset(z[t][:, NODES:Z_COLS], 0.0)

        w_bf = sb.tile([P, PACK, P, PACK], BF16, name="w_bf", tag="w_bf", align_bytes=64)
        w_src = w_raw[:].rearrange("p j (m t) -> p m j t", t=PACK)
        w_dst = w_bf[:].rearrange("p t m j -> p m j t")
        w_codes = sb.tile([P, 512], U32, name="w_codes", align_bytes=64)
        w_scales = sb.tile([P, 512], U8, name="w_scales", align_bytes=64)
        nc.vector.tensor_copy(out=w_dst[:, :, :, 0:2], in_=w_src[:, :, :, 0:2])
        nc.scalar.copy(out=w_dst[:, :, :, 2:4], in_=w_src[:, :, :, 2:4])

        def quantize_w(half):
            c = slice(256 * half, 256 * (half + 1))
            nc.vector.quantize_mx(
                out=w_codes[:, c].bitcast(E4M3),
                scales=w_scales[:, c],
                in_=w_bf[:, 2 * half : 2 * half + 2].rearrange("p t m j -> p (t m j)"),
            )

        h_codes = sb.tile([P, NODES], U32, name="h_codes", align_bytes=64)
        h_scales = sb.tile([P, NODES], U8, name="h_scales", align_bytes=64)
        h_bf = [sb.tile([P, b - a, PACK], BF16, name="h_bf%d" % n, align_bytes=64) for n, (a, b) in enumerate(H_PIECES)]

        def cast_h(n, copy):
            copy(
                out=h_bf[n][:].rearrange("p (c i) j -> p c j i", i=4),
                in_=h_raw[n][:].rearrange("p j (c i) -> p c j i", i=4),
            )

        def quantize_h(n):
            a, b = H_PIECES[n]
            nc.vector.quantize_mx(
                out=h_codes[:, a:b].bitcast(E4M3),
                scales=h_scales[:, a:b],
                in_=h_bf[n][:].rearrange("p x j -> p (x j)"),
            )

        def mx(out_ap, codes_l, scales_l, cl, codes_r, scales_r, cr, fmt_r=E4M3):
            nc.tensor.matmul_mx(
                out=out_ap,
                lhsT=codes_l[:, cl].bitcast(E4M3),
                lhsT_scale=scales_l[:, cl],
                rhs=codes_r[:, cr].bitcast(fmt_r),
                rhs_scale=scales_r[:, cr],
                start=True,
                stop=True,
            )

        def plane0(n, b):
            lo, hi = H_PIECES[n]
            acc = bank(b, "z0_ps%d" % n)
            mx(acc[:, 0 : hi - lo], w_codes, w_scales, slice(0, P), h_codes, h_scales, slice(lo, hi))
            nc.vector.scalar_tensor_tensor(
                out=z[0][:, lo:hi], in0=acc[:, 0 : hi - lo], scalar=cd_cols[:, 0:1], in1=sx_all[:, lo:hi], op0=MULT, op1=MULT
            )

        quantize_w(0)
        cast_h(0, nc.vector.tensor_copy)
        quantize_w(1)
        quantize_h(0)
        cast_h(1, nc.scalar.copy)
        cast_h(2, nc.vector.tensor_copy)
        quantize_h(1)
        quantize_h(2)
        plane0(0, 2)
        plane0(1, 0)
        plane0(2, 1)

        sx_ps = bank(5, "sx_ps")
        for k in range(4):
            nc.tensor.transpose(sx_ps[:, k * P : (k + 1) * P], sx_all[:, k * P : (k + 1) * P], ident[:])
        sx_cols = sb.tile([P, 4], F32, name="sx_cols")
        nc.scalar.copy(out=sx_cols[:], in_=sx_ps[:, 0:NODES:P])
        back = [None] + [bank(4 + t, "z_back%d" % t) for t in range(1, PACK)]
        z_nodes = []
        for k in range(4):
            acc = bank(3 + k % 2, "zt_ps%d" % k)
            nodes = slice(k * P, (k + 1) * P)
            mx(acc[:, 0:128], h_codes, h_scales, nodes, w_codes, w_scales, slice(128, 256))
            mx(acc[:, 128:384], h_codes, h_scales, nodes, w_codes, w_scales, slice(256, 512))
            scaled = sb.tile([P, 384], F32, name="z_nodes%d" % k)
            nc.scalar.activation(out=scaled[:], in_=acc[:, 0:384], func=COPY, scale=sx_cols[:, k : k + 1])
            z_nodes.append(scaled)
        for t in range(1, PACK):
            for k in range(4):
                nc.tensor.transpose(back[t][:, k * P : (k + 1) * P], z_nodes[k][:, (t - 1) * P : t * P], ident[:])
            nc.scalar.activation(out=z[t][:, 0:NODES], in_=back[t][:], func=COPY, scale=cd_cols[:, t : t + 1])

        w_words = w_bf[:].rearrange("p t m j -> p (t m j)").bitcast(F32).rearrange("p (t m u) -> p t m u", t=4, u=2)
        wt_bf = sb.tile([P, PACK, P, PACK], BF16, name="wt_bf", align_bytes=64)
        for u in range(2):
            turned = bank(6 + u, "wt_ps%d" % u)
            for t in range(PACK):
                nc.tensor.transpose(turned[:, t * P : (t + 1) * P], w_words[:, t, :, u], ident[:])
            nc.scalar.copy(
                out=wt_bf[:, 2 * u : 2 * u + 2],
                in_=turned[:].bitcast(BF16).rearrange("m (t p e) -> m e p t", t=4, e=2),
            )
        wt_codes = sb.tile([P, 512], U32, name="wt_codes", align_bytes=64)
        wt_scales = sb.tile([P, 512], U8, name="wt_scales", align_bytes=64)

        rows_t = bank(5, "rows_t")
        nc.tensor.transpose(rows_t[:, 0:P], rows[:], ident[:])
        we_cols = sb.tile([P, 8], F32, name="we_cols")
        nc.scalar.copy(out=we_cols[:], in_=rows_t[:, WE_ROW:Y_ROW])
        neg_wy = sb.tile([P, 8], F32, name="neg_wy")
        nc.vector.scalar_tensor_tensor(
            out=neg_wy[:], in0=rows_t[:, Y_ROW:ROWS_END], scalar=-1.0, in1=we_cols[:], op0=MULT, op1=MULT
        )

        factors = sb.tile([P, 2, PACK, 2 * P], F32, name="factors", tag="w_bf", align_bytes=64)
        nc.scalar.copy(out=factors[:, 0], in_=cd_cols[:].unsqueeze(2).to_broadcast([P, PACK, 2 * P]))
        for t in range(PACK):
            nc.scalar.activation(
                out=factors[:, 1, t, :].rearrange("p (x j) -> p x j", j=2),
                in_=sx_all[:, NODES - P : NODES].unsqueeze(2).to_broadcast([P, P, 2]),
                func=COPY,
                scale=cd_cols[:, t : t + 1],
            )

        z_dst = sb.tile([P, PACK, EDGES], F32, name="z_dst")
        q = sb.tile([P, PACK, EDGES], F32, name="q", tag="q")

        def gather_dst(t, a, b):
            nc.vector.tensor_copy(z_dst[:, t, a:b], z[t][:].indirect(offsets(dst_list, a, b)))

        def gather_src(t, a, b):
            nc.vector.tensor_tensor(q[:, t, a:b], z[t][:].indirect(offsets(src_list, a, b)), z_dst[:, t, a:b], MULT)

        for a in (0, 512):
            gather_dst(0, a, a + 512)
        for a in (0, 512):
            gather_src(0, a, a + 512)

        s = sb.tile([P, 8], F32, name="s")
        sig = sb.tile([P, 8], F32, name="sig")
        g = sb.tile([P, 8], F32, name="g")
        unread = sb.tile([P, 8, P], F32, name="unread")

        def score(n, q_bank):
            a, b = EDGE_PIECES[n]
            gather_dst(1, a, b)
            gather_dst(2, a, b)
            gather_src(1, a, b)
            gather_dst(3, a, b)
            gather_src(2, a, b)
            gather_src(3, a, b)
            q_ps = bank(q_bank, "q_ps%d" % n)
            chunks = range(a // P, b // P)
            for k in chunks:
                part = q_ps[:, k * P - a : (k + 1) * P - a]
                order = (3, 0, 1, 2) if k == 0 else (0, 1, 2, 3)
                for t in order:
                    nc.tensor.matmul(
                        part, q[:, t, k * P : (k + 1) * P], ident[:], start=(t == order[0]), stop=(t == order[3]), is_transpose=True
                    )
            for k in chunks:
                part = q_ps[:, k * P - a : (k + 1) * P - a]
                nc.scalar.activation(out=unread[:, k, :], in_=part, func=IDENTITY, accum_out=s[:, k : k + 1])
            nc.scalar.activation(out=sig[:, a // P : b // P], in_=s[:, a // P : b // P], func=SIGMOID)
            for k in chunks:
                nc.scalar.activation(
                    out=g[:, k : k + 1], in_=sig[:, k : k + 1], func=IDENTITY, scale=we_cols[:, k : k + 1], bias=neg_wy[:, k : k + 1]
                )

        def spread_g(n, g_bank):
            a, b = EDGE_PIECES[n]
            spread = bank(g_bank, "g_ps%d" % n)
            for k in range(a // P, b // P):
                nc.tensor.transpose(spread[:, k * P - a : (k + 1) * P - a], g[:, k : k + 1].to_broadcast([P, P]), ident[:])
            return spread

        g_rows = sb.tile([P, 512], F32, name="g_rows")
        spreads = []
        for n, (a, b) in enumerate(EDGE_PIECES):
            score(n, 0)
            spreads.append(spread_g(n, (5, 6, 7, 2, 1)[n]))
            if b <= 512:
                nc.scalar.copy(out=g_rows[:, a:b], in_=spreads[n][:, 0 : b - a])
            if n == 1:
                nc.vector.quantize_mx(
                    out=wt_codes[:].bitcast(E4M3), scales=wt_scales[:], in_=wt_bf[:].rearrange("m j p t -> m (j p t)")
                )

        m = [sb.tile([P, EDGES], F32, name="m%d" % t, tag=tag) for t, tag in enumerate(("m0", "m1", "z3", "q"))]
        gpsimd_end = (0, 0, 512, 512)
        for t in (2, 3):
            e = gpsimd_end[t]
            nc.gpsimd.tensor_tensor(m[t][:, 0:e], z_dst[:, t, 0:e], g_rows[:, 0:e], MULT)
        for n, (a, b) in enumerate(EDGE_PIECES):
            for t in range(PACK):
                first = max(a, gpsimd_end[t])
                if first < b:
                    nc.vector.tensor_tensor(m[t][:, first:b], z_dst[:, t, first:b], spreads[n][:, first - a : b - a], MULT)

        dv_codes = sb.tile([P, NODES], U32, name="dv_codes", align_bytes=64)
        dv_scales = sb.tile([P, NODES], U8, name="dv_scales", align_bytes=64)
        dv_bf = [sb.tile([P, P * PACK], BF16, name="dv_bf%d" % k, align_bytes=64) for k in range(4)]

        def quantize_dv(k):
            nodes = slice(k * P, (k + 1) * P)
            nc.vector.quantize_mx(out=dv_codes[:, nodes].bitcast(E5M2), scales=dv_scales[:, nodes], in_=dv_bf[k][:])

        def gather_outg(picked, t, k, factor):
            nc.vector.tensor_tensor(picked, m[t][:].indirect(offsets(outg_list, 2 * P * k, 2 * P * (k + 1))), factor, MULT)

        for k in range(3):
            dz_ps = bank(3 + k % 2, "dz_ps%d" % k)
            for t in range(PACK):
                picked = sb.tile([P, 2 * P], F32, name="picked%d_%d" % (k, t))
                gather_outg(picked[:], t, k, factors[:, 0, t, :])
                for j in range(2):
                    nc.tensor.matmul(
                        dz_ps[:, t * P : (t + 1) * P], picked[:, j : 2 * P : 2], ident[:], start=(j == 0), stop=(j == 1), is_transpose=True
                    )
            dv_nodes = sb.tile([P, 2, P, 2], BF16, name="dv_nodes%d" % k)
            nc.scalar.activation(
                out=dv_nodes[:], in_=dz_ps[:].rearrange("x (u e p) -> x u p e", u=2, e=2), func=COPY, scale=sx_cols[:, k : k + 1]
            )
            words = dv_nodes[:].rearrange("x u p e -> x (u p e)").bitcast(F32)
            dv_ps = bank((0, 5)[k % 2], "dv_ps%d" % k)
            for u in range(2):
                nc.tensor.transpose(dv_ps[:, u * P : (u + 1) * P], words[:, u * P : (u + 1) * P], ident[:])
            nc.scalar.copy(
                out=dv_bf[k][:].bitcast(F32).rearrange("p (x u) -> p x u", u=2),
                in_=dv_ps[:, 0 : 2 * P].rearrange("p (u x) -> p x u", u=2),
            )

        picked_last = sb.tile([P, PACK, 2 * P], F32, name="picked_last")
        for t in range(PACK):
            gather_outg(picked_last[:, t, :], t, 3, factors[:, 1, t, :])
        pairs = picked_last[:].rearrange("p t (c i j) -> p c t i j", i=4, j=2)
        quantize_dv(0)
        nc.vector.tensor_tensor(
            dv_bf[3][:].rearrange("p (c i t) -> p c t i", i=4, t=4), pairs[:, :, :, :, 0], pairs[:, :, :, :, 1], ADD
        )
        quantize_dv(1)
        quantize_dv(2)
        quantize_dv(3)

        out_rows = out.rearrange("(p j) x -> p j x", j=PACK)
        for j in range(PACK):
            acc = bank((5, 6, 7, 2)[j], "out_ps%d" % j)
            mx(acc[:], wt_codes, wt_scales, slice(j * P, (j + 1) * P), dv_codes, dv_scales, slice(0, NODES), E5M2)
            result = sb.tile([P, NODES], F32, name="result%d" % j)
            if j % 2 == 0:
                nc.scalar.copy(out=result[:], in_=acc[:])
            else:
                nc.vector.tensor_copy(out=result[:], in_=acc[:])
            nc.sync.dma_start(out=out_rows[:, j, :], in_=result[:])
